import numpy as np, ml_dtypes
CORES = [2,34,66,98,130,162,194,226,258,290,322,354,386,418,450,482]
N = 16
R = 512
def setup_inputs(rng):
    m = (rng.standard_normal((N, 128, 128), dtype=np.float32) / 11).astype(ml_dtypes.bfloat16)
    q = rng.standard_normal((128, R), dtype=np.float32).astype(ml_dtypes.bfloat16)
    return {"m": m, "mt": m.transpose(0, 2, 1).copy(), "q": np.broadcast_to(q, (N, 128, R)).copy()}
def setup_inputs_big(rng):
    d = setup_inputs(rng)
    for k in ("m", "mt", "q"): d[k] = (d[k].astype(np.float32) * 1024.0).astype(d[k].dtype)
    return d
def setup_inputs_small(rng):
    d = setup_inputs(rng)
    for k in ("m", "mt", "q"): d[k] = (d[k].astype(np.float32) * (1 / 1024.0)).astype(d[k].dtype)
    return d
def setup_inputs_apart(rng):
    d = setup_inputs(rng)
    f = (10.0 ** rng.permutation(np.linspace(-1.5, 1.5, N))).astype(np.float32).reshape(N, 1, 1)
    for k in ("m", "mt"): d[k] = (d[k].astype(np.float32) * f).astype(d[k].dtype)
    return d
def tie_inputs(x):
    x = dict(x)
    x["mt"] = x["m"].transpose(0, 2, 1).copy(); x["q"] = np.broadcast_to(x["q"][0], x["q"].shape).copy()
    return x
def reference(m, mt, q):
    M, MT, Q = m.astype(np.float64), mt.astype(np.float64), q.astype(np.float64)
    p = sum(MT[j].T @ Q[j] for j in range(N))
    q2 = sum(M[j].T @ p for j in range(N))
    return {"p": np.broadcast_to(p.astype(ml_dtypes.bfloat16 if m.dtype != np.float64 else np.float64), (N, 128, R)), "q2": np.broadcast_to(q2.astype(ml_dtypes.bfloat16 if m.dtype != np.float64 else np.float64), (N, 128, R))}

@@ -1,0 +1,144 @@
+from concourse.bass import DstId, RemoteDMATransfer
+
+W = 128
+R = 512
+H = R // 2
+BF, F32 = "bfloat16", "float32"
+
+SCRATCH = {
+    "grp":   ("dram", [4, W, W], BF),
+    "eyeD":  ("dram", [W + 1, W], BF),
+    "eyeA":  ("sbuf", [W, W + 1], BF),
+    "eye":   ("sbuf", [W, W], BF),
+    "eye4":  ("sbuf", [W, 4 * W], BF),
+    "blk":   ("sbuf", [W, 4 * W], BF),
+    "land2": ("sbuf", [W, 3 * W], BF),
+    "q_sb":  ("sbuf", [W, R], BF),
+    "st_sb": ("sbuf", [W, W], BF),
+    "s_sb":  ("sbuf", [W, W], BF),
+    "p_sb":  ("sbuf", [W, R], BF),
+    "q2_sb": ("sbuf", [W, R], BF),
+    "ps_st": ("psum", [W, 512], F32),
+    "ps_s":  ("psum", [W, 512], F32),
+    "ps_pa": ("psum", [W, 512], F32),
+    "ps_pb": ("psum", [W, 512], F32),
+    "ps_qa": ("psum", [W, 512], F32),
+    "ps_qb": ("psum", [W, 512], F32),
+}
+SEMAPHORES = ["ld_m", "ld_q", "fill", "e1", "e2", "arr1", "ld_b", "arr2", "sent", "stored",
+              "s_st", "c_st", "s_s", "c_s", "s_pa", "c_pa", "s_pb", "c_pb", "s_qa", "c_qa", "s_qb", "c_qb"]
+
+
+def _plan(core, T, topo):
+    cores = list(T.cores)
+    chips = sorted({topo.chip(c) for c in cores})
+
+    def place(c):
+        return chips.index(topo.chip(c))
+
+    def rack(c):
+        return topo.rack(topo.host(c))
+
+    def square(c):
+        return sorted(d for d in cores if place(d) // 2 == place(c) // 2 and
+                      (topo.host(d) == topo.host(c) or (rack(d) != rack(c) and topo.may_write(c, d))))
+
+    def line(c):
+        return sorted(d for d in cores if rack(d) == rack(c) and place(d) % 2 == place(c) % 2)
+
+    sq, ln = square(core), line(core)
+    assert len(sq) == 4 and len(ln) == 4
+    assert sorted(x for d in ln for x in square(d)) == sorted(cores)
+    assert all(topo.same_plane(core, d) for d in ln if d != core)
+    return sq, ln
+
+
+def _send(g, core, topo, dests, srcs, dsts, alu, remote_sem, local_sem):
+    mask = topo.mask(core, dests[0])
+    for d in dests:
+        mask &= topo.mask(core, d)
+    ids = []
+    for d in dests:
+        rid, pid = topo.addr(d, core)
+        ids.append(DstId(rid=rid, pnc=pid))
+    g.remote_dma_fused([RemoteDMATransfer(dst_ids=ids, dma_engine_mask=mask, remote_sem=remote_sem,
+                                          srcs=srcs, dsts=dsts, alu_op=alu)], local_sem=local_sem)
+    return bin(mask).count("1")
+
+
+def rank_program(g, core, T, topo):
+    if T.rank_of(core) is None:
+        return
+    S = T.sem
+    sq, ln = _plan(core, T, topo)
+    me1, me2 = sq.index(core), ln.index(core)
+
+    g.sync.dma_start(T.grp[me1], T.mt[:, :]).then_inc(S.ld_m, 16)
+    g.sync.dma_start(T.q_sb[:, :], T.q[:, :]).then_inc(S.ld_q, 16)
+
+    g.vector.memset(T.eyeA[:, 0:1], 1.0).then_inc(S.fill, 1)
+    g.vector.memset(T.eyeA[:, 1:W + 1], 0.0).then_inc(S.fill, 1)
+    g.scalar.wait_ge(S.fill, 2)
+    g.scalar.dma_start(T.eyeD[:, :], T.eyeA[:, :]).then_inc(S.e1, 16)
+    g.scalar.wait_ge(S.e1, 16)
+    for k in range(4):
+        g.scalar.dma_start(T.eye4[32 * k:32 * (k + 1), :], T.eyeD[0:W, :]).then_inc(S.e2, 16)
+    g.scalar.dma_start(T.eye[:, :], T.eyeD[0:W, :]).then_inc(S.e2, 16)
+
+    g.wait_ge(S.ld_m, 16)
+    d1 = [d for d in sq if d != core]
+    n1 = _send(g, core, topo, d1, [T.grp[me1]], [T.grp[me1] for _ in d1], 0, S.arr1, S.sent)
+    g.wait_ge(S.arr1, 3 * n1)
+    d2 = [ln[(me2 - 1 - j) % 4] for j in range(3)]
+    n2 = _send(g, core, topo, d2, [T.grp[k] for k in range(4)],
+               [T.land2[:, j * W:(j + 1) * W] for j in range(3)], 1, S.arr2, S.sent)
+
+    g.sync.wait_ge(S.ld_m, 16)
+    g.sync.wait_ge(S.arr1, 3 * n1)
+    g.sync.dma_start(T.blk[:, :], T.grp[:, :, :]).then_inc(S.ld_b, 16)
+
+    te, ve = g.tensor, g.vector
+    st = T.ps_st[:, 0:W]
+    te.wait_ge(S.e2, 80)
+    te.wait_ge(S.ld_b, 16)
+    for c in range(4):
+        te.matmul(st, T.eye4[:, c * W:(c + 1) * W], T.blk[:, c * W:(c + 1) * W], c == 0, False)
+    te.wait_ge(S.arr2, 3 * n2)
+    for k in range(3):
+        mm = te.matmul(st, T.eye[:, :], T.land2[:, k * W:(k + 1) * W], False, k == 2)
+    mm.then_inc(S.s_st, 1)
+    te.wait_ge(S.c_st, 1)
+    te.wait_ge(S.ld_q, 16)
+    te.matmul(T.ps_s[:, 0:W], T.st_sb[:, :], T.eye[:, :], True, True).then_inc(S.s_s, 1)
+    te.matmul(T.ps_pa[:, 0:H], T.st_sb[:, :], T.q_sb[:, 0:H], True, True).then_inc(S.s_pa, 1)
+    te.matmul(T.ps_pb[:, 0:H], T.st_sb[:, :], T.q_sb[:, H:R], True, True).then_inc(S.s_pb, 1)
+    te.wait_ge(S.c_s, 1)
+    te.wait_ge(S.c_pa, 1)
+    te.matmul(T.ps_qa[:, 0:H], T.s_sb[:, :], T.p_sb[:, 0:H], True, True).then_inc(S.s_qa, 1)
+    te.wait_ge(S.c_pb, 1)
+    te.matmul(T.ps_qb[:, 0:H], T.s_sb[:, :], T.p_sb[:, H:R], True, True).then_inc(S.s_qb, 1)
+
+    ve.wait_ge(S.s_st, 1)
+    ve.tensor_copy(T.st_sb[:, :], st).then_inc(S.c_st, 1)
+    ve.wait_ge(S.s_s, 1)
+    ve.tensor_copy(T.s_sb[:, :], T.ps_s[:, 0:W]).then_inc(S.c_s, 1)
+    ve.wait_ge(S.s_pa, 1)
+    ve.tensor_copy(T.p_sb[:, 0:H], T.ps_pa[:, 0:H]).then_inc(S.c_pa, 1)
+    ve.wait_ge(S.s_pb, 1)
+    ve.tensor_copy(T.p_sb[:, H:R], T.ps_pb[:, 0:H]).then_inc(S.c_pb, 1)
+    ve.wait_ge(S.s_qa, 1)
+    ve.tensor_copy(T.q2_sb[:, 0:H], T.ps_qa[:, 0:H]).then_inc(S.c_qa, 1)
+    ve.wait_ge(S.s_qb, 1)
+    ve.tensor_copy(T.q2_sb[:, H:R], T.ps_qb[:, 0:H]).then_inc(S.c_qb, 1)
+
+    g.sync.wait_ge(S.c_pa, 1)
+    g.sync.dma_start(T.p[:, 0:H], T.p_sb[:, 0:H]).then_inc(S.stored, 16)
+    g.scalar.wait_ge(S.c_pb, 1)
+    g.scalar.dma_start(T.p[:, H:R], T.p_sb[:, H:R]).then_inc(S.stored, 16)
+    g.sync.wait_ge(S.c_qa, 1)
+    g.sync.dma_start(T.q2[:, 0:H], T.q2_sb[:, 0:H]).then_inc(S.stored, 16)
+    g.scalar.wait_ge(S.c_qb, 1)
+    g.scalar.dma_start(T.q2[:, H:R], T.q2_sb[:, H:R]).then_inc(S.stored, 16)
+
+    g.wait_ge(S.sent, n1 + n2)
+    g.wait_ge(S.stored, 64)

@@ -3,6 +3,8 @@ from concourse.bass import DstId, RemoteDMATransfer
 W = 128
 R = 512
 H = R // 2
+NC = 4
+C = R // NC
 BF, F32 = "bfloat16", "float32"
 
 SCRATCH = {
@@ -10,23 +12,28 @@ SCRATCH = {
     "eyeD":  ("dram", [W + 1, W], BF),
     "eyeA":  ("sbuf", [W, W + 1], BF),
     "eye":   ("sbuf", [W, W], BF),
-    "eye4":  ("sbuf", [W, 4 * W], BF),
-    "blk":   ("sbuf", [W, 4 * W], BF),
+    "eye2":  ("sbuf", [W, 2 * W], BF),
+    "own":   ("sbuf", [W, W], BF),
+    "early": ("sbuf", [W, 2 * W], BF),
+    "late":  ("sbuf", [W, W], BF),
     "land2": ("sbuf", [W, 3 * W], BF),
     "q_sb":  ("sbuf", [W, R], BF),
     "st_sb": ("sbuf", [W, W], BF),
     "s_sb":  ("sbuf", [W, W], BF),
     "p_sb":  ("sbuf", [W, R], BF),
     "q2_sb": ("sbuf", [W, R], BF),
-    "ps_st": ("psum", [W, 512], F32),
-    "ps_s":  ("psum", [W, 512], F32),
-    "ps_pa": ("psum", [W, 512], F32),
-    "ps_pb": ("psum", [W, 512], F32),
-    "ps_qa": ("psum", [W, 512], F32),
-    "ps_qb": ("psum", [W, 512], F32),
+    "b0": ("psum", [W, 512], F32),
+    "b1": ("psum", [W, 512], F32),
+    "b2": ("psum", [W, 512], F32),
+    "b3": ("psum", [W, 512], F32),
+    "b4": ("psum", [W, 512], F32),
+    "b5": ("psum", [W, 512], F32),
+    "b6": ("psum", [W, 512], F32),
+    "b7": ("psum", [W, 512], F32),
 }
-SEMAPHORES = ["ld_m", "ld_q", "fill", "e1", "e2", "arr1", "ld_b", "arr2", "sent", "stored",
-              "s_st", "c_st", "s_s", "c_s", "s_pa", "c_pa", "s_pb", "c_pb", "s_qa", "c_qa", "s_qb", "c_qb"]
+SEMAPHORES = ["ld_m", "ld_o", "ld_q", "fill", "e1", "e2", "arr1e", "arr1c", "go", "ld_e", "ld_l",
+              "a2_0", "a2_1", "a2_2", "a2_3", "sent", "stored",
+              "s_st", "c_st", "s_s", "c_s"] + ["%s_%s%d" % (x, y, c) for x in "sc" for y in "pq" for c in range(4)]
 
 
 def _plan(core, T, topo):
@@ -53,17 +60,18 @@ def _plan(core, T, topo):
     return sq, ln
 
 
-def _send(g, core, topo, dests, srcs, dsts, alu, remote_sem, local_sem):
-    mask = topo.mask(core, dests[0])
-    for d in dests:
-        mask &= topo.mask(core, d)
+def _send(g, core, topo, dests, engines, srcs, dsts, alu, remote_sem, local_sem):
+    mask = 0
+    for e in engines:
+        mask |= 1 << e
     ids = []
     for d in dests:
+        assert mask & topo.mask(core, d) == mask
         rid, pid = topo.addr(d, core)
         ids.append(DstId(rid=rid, pnc=pid))
     g.remote_dma_fused([RemoteDMATransfer(dst_ids=ids, dma_engine_mask=mask, remote_sem=remote_sem,
                                           srcs=srcs, dsts=dsts, alu_op=alu)], local_sem=local_sem)
-    return bin(mask).count("1")
+    return len(engines)
 
 
 def rank_program(g, core, T, topo):
@@ -71,9 +79,20 @@ def rank_program(g, core, T, topo):
         return
     S = T.sem
     sq, ln = _plan(core, T, topo)
-    me1, me2 = sq.index(core), ln.index(core)
+    me2 = ln.index(core)
+    others = [d for d in sq if d != core]
+    near = [d for d in others if topo.host(d) == topo.host(core)][0]
+    cable = [d for d in others if d != near and topo.chip(d) == topo.chip(core)][0]
+    cross = [d for d in others if d != near and d != cable][0]
+    common = topo.mask(core, near)
+    for d in others + [x for x in ln if x != core]:
+        common &= topo.mask(core, d)
+    eng = [b for b in range(16) if (common >> b) & 1]
+    half, rest = eng[0::2], eng[1::2]
+    k = len(rest) // 2
 
-    g.sync.dma_start(T.grp[me1], T.mt[:, :]).then_inc(S.ld_m, 16)
+    g.sync.dma_start(T.grp[0], T.mt[:, :]).then_inc(S.ld_m, 16)
+    g.sync.dma_start(T.own[:, :], T.mt[:, :]).then_inc(S.ld_o, 16)
     g.sync.dma_start(T.q_sb[:, :], T.q[:, :]).then_inc(S.ld_q, 16)
 
     g.vector.memset(T.eyeA[:, 0:1], 1.0).then_inc(S.fill, 1)
@@ -81,64 +100,77 @@ def rank_program(g, core, T, topo):
     g.scalar.wait_ge(S.fill, 2)
     g.scalar.dma_start(T.eyeD[:, :], T.eyeA[:, :]).then_inc(S.e1, 16)
     g.scalar.wait_ge(S.e1, 16)
-    for k in range(4):
-        g.scalar.dma_start(T.eye4[32 * k:32 * (k + 1), :], T.eyeD[0:W, :]).then_inc(S.e2, 16)
     g.scalar.dma_start(T.eye[:, :], T.eyeD[0:W, :]).then_inc(S.e2, 16)
+    for h in range(2):
+        g.scalar.dma_start(T.eye2[64 * h:64 * (h + 1), :], T.eyeD[0:W, :]).then_inc(S.e2, 16)
 
     g.wait_ge(S.ld_m, 16)
-    d1 = [d for d in sq if d != core]
-    n1 = _send(g, core, topo, d1, [T.grp[me1]], [T.grp[me1] for _ in d1], 0, S.arr1, S.sent)
-    g.wait_ge(S.arr1, 3 * n1)
+    nc = _send(g, core, topo, [cable], half, [T.grp[0]], [T.grp[3]], 0, S.arr1c, S.sent)
+    na = _send(g, core, topo, [near], rest[:k], [T.grp[0]], [T.grp[1]], 0, S.arr1e, S.sent)
+    nb = _send(g, core, topo, [cross], rest[k:], [T.grp[0]], [T.grp[2]], 0, S.arr1e, S.sent)
+    g.wait_ge(S.arr1e, na + nb)
+    g.wait_ge(S.arr1c, nc)
     d2 = [ln[(me2 - 1 - j) % 4] for j in range(3)]
-    n2 = _send(g, core, topo, d2, [T.grp[k] for k in range(4)],
-               [T.land2[:, j * W:(j + 1) * W] for j in range(3)], 1, S.arr2, S.sent)
+    n2 = _send(g, core, topo, d2, eng, [T.grp[s] for s in range(4)],
+               [T.land2[:, j * W:(j + 1) * W] for j in range(3)], 1, S["a2_%d" % me2], S.sent)
+    g.sem_inc(S.go, 1)
 
-    g.sync.wait_ge(S.ld_m, 16)
-    g.sync.wait_ge(S.arr1, 3 * n1)
-    g.sync.dma_start(T.blk[:, :], T.grp[:, :, :]).then_inc(S.ld_b, 16)
+    g.sync.wait_ge(S.arr1e, na + nb)
+    g.sync.dma_start(T.early[:, :], T.grp[1:3]).then_inc(S.ld_e, 16)
+    g.sync.wait_ge(S.arr1c, nc)
+    g.sync.wait_ge(S.go, 1)
+    g.sync.dma_start(T.late[:, :], T.grp[3]).then_inc(S.ld_l, 16)
 
     te, ve = g.tensor, g.vector
-    st = T.ps_st[:, 0:W]
-    te.wait_ge(S.e2, 80)
-    te.wait_ge(S.ld_b, 16)
-    for c in range(4):
-        te.matmul(st, T.eye4[:, c * W:(c + 1) * W], T.blk[:, c * W:(c + 1) * W], c == 0, False)
-    te.wait_ge(S.arr2, 3 * n2)
-    for k in range(3):
-        mm = te.matmul(st, T.eye[:, :], T.land2[:, k * W:(k + 1) * W], False, k == 2)
-    mm.then_inc(S.s_st, 1)
+    st, ss = T.b0[:, 0:W], T.b1[:, 0:W]
+
+    def add(sel, x, first, last):
+        a1 = te.matmul(st, sel, x, first, last)
+        a2 = te.matmul(ss, x, sel, first, last)
+        return a1, a2
+
+    te.wait_ge(S.e2, 48)
+    te.wait_ge(S.ld_o, 16)
+    add(T.eye[:, :], T.own[:, :], True, False)
+    te.wait_ge(S.ld_e, 16)
+    for c in range(2):
+        add(T.eye2[:, c * W:(c + 1) * W], T.early[:, c * W:(c + 1) * W], False, False)
+    for j in range(2):
+        te.wait_ge(S["a2_%d" % ((me2 + 1 + j) % 4)], n2)
+        add(T.eye[:, :], T.land2[:, j * W:(j + 1) * W], False, False)
+    te.wait_ge(S.ld_l, 16)
+    add(T.eye[:, :], T.late[:, :], False, False)
+    te.wait_ge(S["a2_%d" % ((me2 + 3) % 4)], n2)
+    a1, a2 = add(T.eye[:, :], T.land2[:, 2 * W:3 * W], False, True)
+    a1.then_inc(S.s_st, 1)
+    a2.then_inc(S.s_s, 1)
+    pb = [T.b2, T.b3, T.b4, T.b5]
+    qb = [T.b6, T.b7, T.b0, T.b1]
     te.wait_ge(S.c_st, 1)
     te.wait_ge(S.ld_q, 16)
-    te.matmul(T.ps_s[:, 0:W], T.st_sb[:, :], T.eye[:, :], True, True).then_inc(S.s_s, 1)
-    te.matmul(T.ps_pa[:, 0:H], T.st_sb[:, :], T.q_sb[:, 0:H], True, True).then_inc(S.s_pa, 1)
-    te.matmul(T.ps_pb[:, 0:H], T.st_sb[:, :], T.q_sb[:, H:R], True, True).then_inc(S.s_pb, 1)
+    for c in range(NC):
+        te.matmul(pb[c][:, 0:C], T.st_sb[:, :], T.q_sb[:, c * C:(c + 1) * C], True, True).then_inc(S["s_p%d" % c], 1)
     te.wait_ge(S.c_s, 1)
-    te.wait_ge(S.c_pa, 1)
-    te.matmul(T.ps_qa[:, 0:H], T.s_sb[:, :], T.p_sb[:, 0:H], True, True).then_inc(S.s_qa, 1)
-    te.wait_ge(S.c_pb, 1)
-    te.matmul(T.ps_qb[:, 0:H], T.s_sb[:, :], T.p_sb[:, H:R], True, True).then_inc(S.s_qb, 1)
+    for c in range(NC):
+        te.wait_ge(S["c_p%d" % c], 1)
+        te.matmul(qb[c][:, 0:C], T.s_sb[:, :], T.p_sb[:, c * C:(c + 1) * C], True, True).then_inc(S["s_q%d" % c], 1)
 
     ve.wait_ge(S.s_st, 1)
     ve.tensor_copy(T.st_sb[:, :], st).then_inc(S.c_st, 1)
     ve.wait_ge(S.s_s, 1)
-    ve.tensor_copy(T.s_sb[:, :], T.ps_s[:, 0:W]).then_inc(S.c_s, 1)
-    ve.wait_ge(S.s_pa, 1)
-    ve.tensor_copy(T.p_sb[:, 0:H], T.ps_pa[:, 0:H]).then_inc(S.c_pa, 1)
-    ve.wait_ge(S.s_pb, 1)
-    ve.tensor_copy(T.p_sb[:, H:R], T.ps_pb[:, 0:H]).then_inc(S.c_pb, 1)
-    ve.wait_ge(S.s_qa, 1)
-    ve.tensor_copy(T.q2_sb[:, 0:H], T.ps_qa[:, 0:H]).then_inc(S.c_qa, 1)
-    ve.wait_ge(S.s_qb, 1)
-    ve.tensor_copy(T.q2_sb[:, H:R], T.ps_qb[:, 0:H]).then_inc(S.c_qb, 1)
+    ve.tensor_copy(T.s_sb[:, :], ss).then_inc(S.c_s, 1)
+    for c in range(NC):
+        ve.wait_ge(S["s_p%d" % c], 1)
+        ve.tensor_copy(T.p_sb[:, c * C:(c + 1) * C], pb[c][:, 0:C]).then_inc(S["c_p%d" % c], 1)
+    for c in range(NC):
+        ve.wait_ge(S["s_q%d" % c], 1)
+        ve.tensor_copy(T.q2_sb[:, c * C:(c + 1) * C], qb[c][:, 0:C]).then_inc(S["c_q%d" % c], 1)
 
-    g.sync.wait_ge(S.c_pa, 1)
-    g.sync.dma_start(T.p[:, 0:H], T.p_sb[:, 0:H]).then_inc(S.stored, 16)
-    g.scalar.wait_ge(S.c_pb, 1)
-    g.scalar.dma_start(T.p[:, H:R], T.p_sb[:, H:R]).then_inc(S.stored, 16)
-    g.sync.wait_ge(S.c_qa, 1)
-    g.sync.dma_start(T.q2[:, 0:H], T.q2_sb[:, 0:H]).then_inc(S.stored, 16)
-    g.scalar.wait_ge(S.c_qb, 1)
-    g.scalar.dma_start(T.q2[:, H:R], T.q2_sb[:, H:R]).then_inc(S.stored, 16)
+    for name, out, sb in (("c_p%d", T.p, T.p_sb), ("c_q%d", T.q2, T.q2_sb)):
+        for h, queue in enumerate((g.sync, g.scalar)):
+            for c in range(h * NC // 2, (h + 1) * NC // 2):
+                queue.wait_ge(S[name % c], 1)
+            queue.dma_start(out[:, h * H:(h + 1) * H], sb[:, h * H:(h + 1) * H]).then_inc(S.stored, 16)
 
-    g.wait_ge(S.sent, n1 + n2)
+    g.wait_ge(S.sent, nc + na + nb + n2)
     g.wait_ge(S.stored, 64)

from concourse.bass import DstId, RemoteDMATransfer

W = 128
R = 512
H = R // 2
NC = 4
C = R // NC
BF, F32 = "bfloat16", "float32"

SCRATCH = {
    "grp":   ("dram", [4, W, W], BF),
    "eyeD":  ("dram", [W + 1, W], BF),
    "eyeA":  ("sbuf", [W, W + 1], BF),
    "eye":   ("sbuf", [W, W], BF),
    "eye2":  ("sbuf", [W, 2 * W], BF),
    "own":   ("sbuf", [W, W], BF),
    "early": ("sbuf", [W, 2 * W], BF),
    "late":  ("sbuf", [W, W], BF),
    "land2": ("sbuf", [W, 3 * W], BF),
    "q_sb":  ("sbuf", [W, R], BF),
    "st_sb": ("sbuf", [W, W], BF),
    "s_sb":  ("sbuf", [W, W], BF),
    "p_sb":  ("sbuf", [W, R], BF),
    "q2_sb": ("sbuf", [W, R], BF),
    "b0": ("psum", [W, 512], F32),
    "b1": ("psum", [W, 512], F32),
    "b2": ("psum", [W, 512], F32),
    "b3": ("psum", [W, 512], F32),
    "b4": ("psum", [W, 512], F32),
    "b5": ("psum", [W, 512], F32),
    "b6": ("psum", [W, 512], F32),
    "b7": ("psum", [W, 512], F32),
}
SEMAPHORES = ["ld_m", "ld_o", "ld_q", "fill", "e1", "e2", "arr1e", "arr1c", "go", "ld_e", "ld_l",
              "a2_0", "a2_1", "a2_2", "a2_3", "sent", "stored",
              "s_st", "c_st", "s_s", "c_s"] + ["%s_%s%d" % (x, y, c) for x in "sc" for y in "pq" for c in range(4)]


def _plan(core, T, topo):
    cores = list(T.cores)
    chips = sorted({topo.chip(c) for c in cores})

    def place(c):
        return chips.index(topo.chip(c))

    def rack(c):
        return topo.rack(topo.host(c))

    def square(c):
        return sorted(d for d in cores if place(d) // 2 == place(c) // 2 and
                      (topo.host(d) == topo.host(c) or (rack(d) != rack(c) and topo.may_write(c, d))))

    def line(c):
        return sorted(d for d in cores if rack(d) == rack(c) and place(d) % 2 == place(c) % 2)

    sq, ln = square(core), line(core)
    assert len(sq) == 4 and len(ln) == 4
    assert sorted(x for d in ln for x in square(d)) == sorted(cores)
    assert all(topo.same_plane(core, d) for d in ln if d != core)
    return sq, ln


def _send(g, core, topo, dests, engines, srcs, dsts, alu, remote_sem, local_sem):
    mask = 0
    for e in engines:
        mask |= 1 << e
    ids = []
    for d in dests:
        assert mask & topo.mask(core, d) == mask
        rid, pid = topo.addr(d, core)
        ids.append(DstId(rid=rid, pnc=pid))
    g.remote_dma_fused([RemoteDMATransfer(dst_ids=ids, dma_engine_mask=mask, remote_sem=remote_sem,
                                          srcs=srcs, dsts=dsts, alu_op=alu)], local_sem=local_sem)
    return len(engines)


def rank_program(g, core, T, topo):
    if T.rank_of(core) is None:
        return
    S = T.sem
    sq, ln = _plan(core, T, topo)
    me2 = ln.index(core)
    others = [d for d in sq if d != core]
    near = [d for d in others if topo.host(d) == topo.host(core)][0]
    cable = [d for d in others if d != near and topo.chip(d) == topo.chip(core)][0]
    cross = [d for d in others if d != near and d != cable][0]
    common = topo.mask(core, near)
    for d in others + [x for x in ln if x != core]:
        common &= topo.mask(core, d)
    eng = [b for b in range(16) if (common >> b) & 1]
    half, rest = eng[0::2], eng[1::2]
    k = len(rest) // 2

    g.sync.dma_start(T.grp[0], T.mt[:, :]).then_inc(S.ld_m, 16)
    g.sync.dma_start(T.own[:, :], T.mt[:, :]).then_inc(S.ld_o, 16)
    g.sync.dma_start(T.q_sb[:, :], T.q[:, :]).then_inc(S.ld_q, 16)

    g.vector.memset(T.eyeA[:, 0:1], 1.0).then_inc(S.fill, 1)
    g.vector.memset(T.eyeA[:, 1:W + 1], 0.0).then_inc(S.fill, 1)
    g.scalar.wait_ge(S.fill, 2)
    g.scalar.dma_start(T.eyeD[:, :], T.eyeA[:, :]).then_inc(S.e1, 16)
    g.scalar.wait_ge(S.e1, 16)
    g.scalar.dma_start(T.eye[:, :], T.eyeD[0:W, :]).then_inc(S.e2, 16)
    for h in range(2):
        g.scalar.dma_start(T.eye2[64 * h:64 * (h + 1), :], T.eyeD[0:W, :]).then_inc(S.e2, 16)

    g.wait_ge(S.ld_m, 16)
    nc = _send(g, core, topo, [cable], half, [T.grp[0]], [T.grp[3]], 0, S.arr1c, S.sent)
    na = _send(g, core, topo, [near], rest[:k], [T.grp[0]], [T.grp[1]], 0, S.arr1e, S.sent)
    nb = _send(g, core, topo, [cross], rest[k:], [T.grp[0]], [T.grp[2]], 0, S.arr1e, S.sent)
    g.wait_ge(S.arr1e, na + nb)
    g.wait_ge(S.arr1c, nc)
    d2 = [ln[(me2 - 1 - j) % 4] for j in range(3)]
    n2 = _send(g, core, topo, d2, eng, [T.grp[s] for s in range(4)],
               [T.land2[:, j * W:(j + 1) * W] for j in range(3)], 1, S["a2_%d" % me2], S.sent)
    g.sem_inc(S.go, 1)

    g.sync.wait_ge(S.arr1e, na + nb)
    g.sync.dma_start(T.early[:, :], T.grp[1:3]).then_inc(S.ld_e, 16)
    g.sync.wait_ge(S.arr1c, nc)
    g.sync.wait_ge(S.go, 1)
    g.sync.dma_start(T.late[:, :], T.grp[3]).then_inc(S.ld_l, 16)

    te, ve = g.tensor, g.vector
    st, ss = T.b0[:, 0:W], T.b1[:, 0:W]

    def add(sel, x, first, last):
        a1 = te.matmul(st, sel, x, first, last)
        a2 = te.matmul(ss, x, sel, first, last)
        return a1, a2

    te.wait_ge(S.e2, 48)
    te.wait_ge(S.ld_o, 16)
    add(T.eye[:, :], T.own[:, :], True, False)
    te.wait_ge(S.ld_e, 16)
    for c in range(2):
        add(T.eye2[:, c * W:(c + 1) * W], T.early[:, c * W:(c + 1) * W], False, False)
    for j in range(2):
        te.wait_ge(S["a2_%d" % ((me2 + 1 + j) % 4)], n2)
        add(T.eye[:, :], T.land2[:, j * W:(j + 1) * W], False, False)
    te.wait_ge(S.ld_l, 16)
    add(T.eye[:, :], T.late[:, :], False, False)
    te.wait_ge(S["a2_%d" % ((me2 + 3) % 4)], n2)
    a1, a2 = add(T.eye[:, :], T.land2[:, 2 * W:3 * W], False, True)
    a1.then_inc(S.s_st, 1)
    a2.then_inc(S.s_s, 1)
    pb = [T.b2, T.b3, T.b4, T.b5]
    qb = [T.b6, T.b7, T.b0, T.b1]
    te.wait_ge(S.c_st, 1)
    te.wait_ge(S.ld_q, 16)
    for c in range(NC):
        te.matmul(pb[c][:, 0:C], T.st_sb[:, :], T.q_sb[:, c * C:(c + 1) * C], True, True).then_inc(S["s_p%d" % c], 1)
    te.wait_ge(S.c_s, 1)
    for c in range(NC):
        te.wait_ge(S["c_p%d" % c], 1)
        te.matmul(qb[c][:, 0:C], T.s_sb[:, :], T.p_sb[:, c * C:(c + 1) * C], True, True).then_inc(S["s_q%d" % c], 1)

    ve.wait_ge(S.s_st, 1)
    ve.tensor_copy(T.st_sb[:, :], st).then_inc(S.c_st, 1)
    ve.wait_ge(S.s_s, 1)
    ve.tensor_copy(T.s_sb[:, :], ss).then_inc(S.c_s, 1)
    for c in range(NC):
        ve.wait_ge(S["s_p%d" % c], 1)
        ve.tensor_copy(T.p_sb[:, c * C:(c + 1) * C], pb[c][:, 0:C]).then_inc(S["c_p%d" % c], 1)
    for c in range(NC):
        ve.wait_ge(S["s_q%d" % c], 1)
        ve.tensor_copy(T.q2_sb[:, c * C:(c + 1) * C], qb[c][:, 0:C]).then_inc(S["c_q%d" % c], 1)

    for name, out, sb in (("c_p%d", T.p, T.p_sb), ("c_q%d", T.q2, T.q2_sb)):
        for h, queue in enumerate((g.sync, g.scalar)):
            for c in range(h * NC // 2, (h + 1) * NC // 2):
                queue.wait_ge(S[name % c], 1)
            queue.dma_start(out[:, h * H:(h + 1) * H], sb[:, h * H:(h + 1) * H]).then_inc(S.stored, 16)

    g.wait_ge(S.sent, nc + na + nb + n2)
    g.wait_ge(S.stored, 64)
